import numpy as np
import ml_dtypes


def mxq(x, axis, fmt="e4m3"):
    dtype, down = {"e4m3": (ml_dtypes.float8_e4m3fn, 7), "e5m2": (ml_dtypes.float8_e5m2, 14)}[fmt]
    v = np.moveaxis(np.asarray(x, np.float32).astype(ml_dtypes.bfloat16).astype(np.float64), axis, -1)
    blocks = v.reshape(v.shape[:-1] + (-1, 32))
    amax = np.abs(blocks).max(-1, keepdims=True)
    byte = np.maximum(np.where(amax > 0, np.frexp(amax)[1] - 1 + 127, 0) - down, 1)
    scale = np.exp2(byte - 127.0)
    codes = (blocks / scale).astype(np.float32).astype(dtype).astype(np.float64)
    return np.moveaxis((codes * scale).reshape(v.shape), -1, axis)


WIDE = False


def mx_kscale(k):
    if not WIDE:
        return np.ones(k)
    levels = np.array([10, -10, 5, -5, 0])
    if k % 512:
        return np.exp2(np.random.permutation(np.resize(levels, k // 32))).repeat(32)
    a = np.empty((k // 512, 16))
    for p in range(k // 512):
        a[p, :8] = np.random.permutation(np.resize(levels, 8))
        for g in range(8):
            far = levels[np.abs(levels - a[p, g]) >= 10]
            a[p, g + 8] = far[np.random.randint(len(far))]
    return np.exp2(a.ravel()).repeat(32)


def f64(x):
    return np.asarray(x).astype(np.float64)


def striped(idx):
    return np.tile(idx.reshape(-1, 16).T, (8, 1)).astype(np.uint16)


def unstriped(offs):
    return offs[:16].T.reshape(-1).astype(np.int64)


def striped8(idx):
    return np.concatenate([x.reshape(-1, 16).T for x in idx]).astype(np.uint16)


def runs(offs, k):
    lists = np.stack([offs[16 * r : 16 * r + 16].T.reshape(-1) for r in range(8)]).astype(np.int64)
    return lists[np.arange(k) % 512 // 64]


def pack_weight(w):
    k, n = w.shape
    w = f64(np.asarray(w, np.float32).astype(ml_dtypes.bfloat16)).reshape(k // 32, 32, n)
    amax = np.abs(w).max(1)
    byte = np.clip(np.where(amax > 0, np.frexp(amax)[1] - 1 + 127 - 7, 1), 1, 254)
    scaled = (w * np.exp2(127.0 - byte)[:, None, :]).reshape(k, n).astype(np.float32)
    words = np.ascontiguousarray(scaled.reshape(k // 512, 128, 4, n).transpose(0, 1, 3, 2)).astype(ml_dtypes.float8_e4m3fn).view(np.uint8)
    return words, np.ascontiguousarray(byte.astype(np.uint8).reshape(k // 512, 16, n))


def unpack_weight(words, scales):
    g, p, n, _ = words.shape
    vals = np.ascontiguousarray(words).view(ml_dtypes.float8_e4m3fn).astype(np.float64) * np.repeat(np.exp2(scales.astype(np.float64) - 127.0), 8, axis=1)[..., None]
    return vals.transpose(0, 1, 3, 2).reshape(g * 512, n)


K, T, S, H, C = 512, 2048, 512, 512, 512


def setup_inputs():
    n = np.random.standard_normal
    s = mx_kscale(K)[:, None]
    packed_xT = pack_weight(n((K, T)) * s)
    return {
        "x_words": packed_xT[0],
        "x_scales": packed_xT[1],
        "w1": (n((K, H)) / np.sqrt(K) / s).astype(np.float32),
        "gs": (np.random.uniform(0.5, 1.5, (K, 1)) / s).astype(np.float32),
        "offs": striped(np.random.permutation(T)[:S]),
        "n1": striped8(np.stack([np.random.permutation(S) for _ in range(8)])),
        "n2": striped8(np.stack([np.random.permutation(S) for _ in range(8)])),
        "ca": striped(np.random.permutation(T)[:C]),
        "cb": striped(np.random.permutation(T)[:C]),
        "n3": striped8(np.stack([np.random.permutation(S) for _ in range(8)])),
        "n4": striped8(np.stack([np.random.permutation(S) for _ in range(8)])),
    }


def reference(x_words, x_scales, w1, gs, offs, n1, n2, ca, cb, n3, n4):
    x_ca = unpack_weight(x_words, x_scales)[:, unstriped(ca)]
    xq = unpack_weight(x_words, x_scales)[:, unstriped(offs)]
    y = mxq(f64(w1), 0, "e4m3").T @ xq
    z = f64(gs) * (y[np.arange(H)[:, None], runs(n1, H)] + 0.75 * (y[np.arange(H)[:, None], runs(n2, H)]))
    zq = mxq(z, 0, "e4m3")
    a = 0.0625 * (x_ca.T @ zq)
    x_cb = unpack_weight(x_words, x_scales)[:, unstriped(cb)]
    b = 0.0625 * (x_cb.T @ zq)
    return np.maximum(a, b[np.arange(C)[:, None], runs(n4, C)]) - (np.minimum(a[np.arange(C)[:, None], runs(n3, C)], b))

@@ -1,0 +1,177 @@
+from contextlib import ExitStack
+
+import concourse.mybir as mybir
+
+K, T, S, H, C = 512, 2048, 512, 512, 512
+FLOPS = 3 * 2 * 512 * 512 * 512
+
+F32 = mybir.dt.float32
+BF16 = mybir.dt.bfloat16
+I32 = mybir.dt.int32
+U32 = mybir.dt.uint32
+U16 = mybir.dt.uint16
+U8 = mybir.dt.uint8
+FP8X4 = mybir.dt.float8_e4m3fn_x4
+ALU = mybir.AluOpType
+COPY = mybir.ActivationFunctionType.Copy
+
+P = 128
+PACK = 4
+HALF = 256
+W_PIECES = ((0, 384), (384, 128))
+Z_PIECES = ((0, 256), (256, 256))
+
+
+def entries(offsets, start, count):
+    return offsets[:, start // 16 : (start + count) // 16]
+
+
+def tile_picked_ccmpmaxbsum_none_p_kernel(
+    tc, x_words, x_scales, w1, gs, offs, n1, n2, ca, cb, n3, n4, out
+):
+    nc = tc.nc
+    with ExitStack() as ctx:
+        keep = ctx.enter_context(tc.tile_pool(name="keep", bufs=1))
+        shared = ctx.enter_context(tc.tile_pool(name="shared", bufs=1))
+        ring = ctx.enter_context(tc.tile_pool(name="ring", bufs=3))
+        psum = ctx.enter_context(tc.psum_pool(name="psum", bufs=1))
+
+        def load_list(name, src):
+            tile = keep.tile([P, S // 16], U16, name=name)
+            nc.sync.dma_start(tile[:], src)
+            return tile
+
+        table_scales = keep.tile([P, T], U8, name="table_scales", align_bytes=64)
+        nc.vector.memset(table_scales[:].bitcast(I32), 0)
+
+        for r in range(4):
+            nc.gpsimd.dma_start(table_scales[r:P:32, :].bitcast(I32), x_scales[0][r:16:4, :].bitcast(I32))
+        gs_sb = keep.tile([P, PACK], F32, name="gs_sb")
+        nc.gpsimd.dma_start(gs_sb[:], gs.rearrange("(p t) o -> p (t o)", t=PACK))
+
+        offs_sb = load_list("offs_sb", offs)
+        table_words = keep.tile([P, T], U32, name="table_words", align_bytes=64)
+        nc.scalar.dma_start(
+            table_words[:].bitcast(I32), x_words[0].rearrange("p n t -> p (n t)").bitcast(I32)
+        )
+        w_rows = w1.rearrange("(p j) c -> p j c", j=PACK)
+        w_raw = []
+        for h, (start, width) in enumerate(W_PIECES):
+            raw = keep.tile([P, PACK, width], F32, name=f"w_raw{h}")
+            nc.scalar.dma_start(raw[:], w_rows[:, :, start : start + width])
+            w_raw.append(raw)
+        ca_sb = load_list("ca_sb", ca)
+        cb_sb = load_list("cb_sb", cb)
+        n2_sb = load_list("n2_sb", n2)
+        n1_sb = load_list("n1_sb", n1)
+        n4_sb = load_list("n4_sb", n4)
+        n3_sb = load_list("n3_sb", n3)
+
+        def gather_dealt(dst, table, offsets):
+            nc.vector.tensor_copy(dst[:].rearrange("p (t m) -> p m t", t=PACK), table[:].indirect(offsets[:]))
+
+        tok_words = keep.tile([P, S], U32, name="tok_words", align_bytes=64)
+        nc.vector.tensor_copy(tok_words[:], table_words[:].indirect(offs_sb[:]))
+        tok_scales = keep.tile([P, S], U8, name="tok_scales", align_bytes=64)
+        nc.vector.tensor_copy(tok_scales[:], table_scales[:].indirect(offs_sb[:]))
+        a_words = keep.tile([P, C], U32, name="a_words", align_bytes=64)
+        gather_dealt(a_words, table_words, ca_sb)
+
+        w_bf = shared.tile([P, H * PACK], BF16, name="w_bf", align_bytes=64, offset=0)
+        w_bf_view = w_bf[:].rearrange("p (t m j) -> p m j t", t=PACK, j=PACK)
+        for h, (start, width) in enumerate(W_PIECES):
+            nc.scalar.activation(
+                w_bf_view[:, start // PACK : (start + width) // PACK],
+                w_raw[h][:].rearrange("p j (m t) -> p m j t", t=PACK),
+                COPY,
+            )
+        w_codes = keep.tile([P, H], U32, name="w_codes", align_bytes=64)
+        w_scales = keep.tile([P, H], U8, name="w_scales", align_bytes=64)
+        for t in range(PACK):
+            rows = slice(t * P, (t + 1) * P)
+            nc.vector.quantize_mx(
+                out=w_codes[:, rows].bitcast(FP8X4), scales=w_scales[:, rows], in_=w_bf[:, t * H : (t + 1) * H]
+            )
+
+        y_sb = [keep.tile([P, S], F32, name=f"y_sb{t}") for t in range(PACK)]
+        for t in range(PACK):
+            rows = slice(t * P, (t + 1) * P)
+            bank = psum.tile([P, S], F32, name=f"y_ps{t}", tag=f"bank{PACK + t}")
+            nc.tensor.matmul_mx(
+                bank[:],
+                lhsT=w_codes[:, rows].bitcast(FP8X4),
+                lhsT_scale=w_scales[:, rows],
+                rhs=tok_words[:].bitcast(FP8X4),
+                rhs_scale=tok_scales[:],
+                start=True,
+                stop=True,
+            )
+            nc.scalar.activation(y_sb[t][:], bank[:], COPY, scale=gs_sb[:, t : t + 1])
+
+        b_words = shared.tile([P, C], U32, name="b_words", align_bytes=64, offset=0)
+        gather_dealt(b_words, table_words, cb_sb)
+        b_scales = shared.tile([P, C], U8, name="b_scales", align_bytes=64, offset=2048)
+        gather_dealt(b_scales, table_scales, cb_sb)
+        a_scales = shared.tile([P, C], U8, name="a_scales", align_bytes=64, offset=3072)
+        gather_dealt(a_scales, table_scales, ca_sb)
+
+        a_ps = [psum.tile([P, S], F32, name=f"a_ps{t}", tag=f"bank{2 * t}") for t in range(PACK)]
+        b_ps = [psum.tile([P, S], F32, name=f"b_ps{t}", tag=f"bank{2 * t + 1}") for t in range(PACK)]
+        a_sb = [keep.tile([P, S], F32, name=f"a_sb{t}") for t in range(PACK)]
+        b_sb = [keep.tile([P, S], F32, name=f"b_sb{t}") for t in range(PACK)]
+
+        for piece, (start, width) in enumerate(Z_PIECES):
+            cols = slice(start, start + width)
+            z_f32 = keep.tile([P, PACK, width], F32, name=f"z_f32_{piece}")
+            for t in range(PACK):
+                second = keep.tile([P, width], F32, name=f"second{piece}{t}")
+                nc.scalar.activation(second[:], y_sb[t][:].indirect(entries(n2_sb, start, width)), COPY, scale=0.75)
+                nc.vector.tensor_tensor(
+                    z_f32[:, t, :], y_sb[t][:].indirect(entries(n1_sb, start, width)), second[:], ALU.add
+                )
+            z_bf = keep.tile([P, width * PACK], BF16, name=f"z_bf{piece}", align_bytes=64)
+            nc.vector.tensor_copy(
+                z_bf[:].rearrange("p (c i t) -> p c t i", i=4, t=PACK),
+                z_f32[:].rearrange("p t (c i) -> p c t i", i=4),
+            )
+            z_codes = keep.tile([P, width], U32, name=f"z_codes{piece}", align_bytes=64)
+            z_scales = keep.tile([P, width], U8, name=f"z_scales{piece}", align_bytes=64)
+            nc.vector.quantize_mx(out=z_codes[:].bitcast(FP8X4), scales=z_scales[:], in_=z_bf[:])
+            for t in range(PACK):
+                rows = slice(t * P, (t + 1) * P)
+                for words, scales, bank, held in (
+                    (b_words, b_scales, b_ps[t], b_sb[t]),
+                    (a_words, a_scales, a_ps[t], a_sb[t]),
+                ):
+                    nc.tensor.matmul_mx(
+                        bank[:, cols],
+                        lhsT=words[:, rows].bitcast(FP8X4),
+                        lhsT_scale=scales[:, rows],
+                        rhs=z_codes[:].bitcast(FP8X4),
+                        rhs_scale=z_scales[:],
+                        start=True,
+                        stop=True,
+                    )
+                    if piece + 1 < len(Z_PIECES):
+                        nc.scalar.activation(held[:, cols], bank[:, cols], COPY, scale=0.0625)
+                    else:
+                        nc.vector.tensor_scalar_mul(held[:, cols], bank[:, cols], 0.0625)
+
+        out_rows = out.rearrange("(p t) j -> p t j", t=PACK)
+        for t in range(PACK):
+            result = keep.tile([P, S], F32, name=f"result{t}")
+            for h in range(2):
+                cols = slice(h * HALF, (h + 1) * HALF)
+                b_at = ring.tile([P, HALF], F32, name="b_at")
+                nc.scalar.activation(b_at[:], b_sb[t][:].indirect(entries(n4_sb, h * HALF, HALF)), COPY)
+                a_at = ring.tile([P, HALF], F32, name="a_at")
+                nc.scalar.activation(a_at[:], a_sb[t][:].indirect(entries(n3_sb, h * HALF, HALF)), COPY)
+                larger = ring.tile([P, HALF], F32, name="larger")
+                nc.vector.tensor_tensor(larger[:], a_sb[t][:, cols], b_at[:], ALU.max)
+                smaller = ring.tile([P, HALF], F32, name="smaller")
+                nc.vector.tensor_tensor(smaller[:], a_at[:], b_sb[t][:, cols], ALU.min)
+                nc.vector.tensor_tensor(result[:, cols], larger[:], smaller[:], ALU.subtract)
+                if t == PACK - 1:
+                    nc.sync.dma_start(out_rows[:, t, cols], result[:, cols])
+            if t < PACK - 1:
+                nc.sync.dma_start(out_rows[:, t, :], result[:])

@@ -18,7 +18,8 @@ COPY = mybir.ActivationFunctionType.Copy
 P = 128
 PACK = 4
 HALF = 256
-W_PIECES = ((0, 384), (384, 128))
+OUT_PIECES = ((0, 256), (256, 256))
+LAST_PIECES = ((0, 256), (256, 128), (384, 128))
 Z_PIECES = ((0, 256), (256, 256))
 
 
@@ -32,8 +33,7 @@ def tile_picked_ccmpmaxbsum_none_p_kernel(
     nc = tc.nc
     with ExitStack() as ctx:
         keep = ctx.enter_context(tc.tile_pool(name="keep", bufs=1))
-        shared = ctx.enter_context(tc.tile_pool(name="shared", bufs=1))
-        ring = ctx.enter_context(tc.tile_pool(name="ring", bufs=3))
+        ring = ctx.enter_context(tc.tile_pool(name="ring", bufs=4))
         psum = ctx.enter_context(tc.psum_pool(name="psum", bufs=1))
 
         def load_list(name, src):
@@ -44,24 +44,22 @@ def tile_picked_ccmpmaxbsum_none_p_kernel(
         table_scales = keep.tile([P, T], U8, name="table_scales", align_bytes=64)
         nc.vector.memset(table_scales[:].bitcast(I32), 0)
 
-        for r in range(4):
-            nc.gpsimd.dma_start(table_scales[r:P:32, :].bitcast(I32), x_scales[0][r:16:4, :].bitcast(I32))
         gs_sb = keep.tile([P, PACK], F32, name="gs_sb")
         nc.gpsimd.dma_start(gs_sb[:], gs.rearrange("(p t) o -> p (t o)", t=PACK))
 
+        for r in range(4):
+            nc.scalar.dma_start(table_scales[r:P:32, :].bitcast(I32), x_scales[0][r:16:4, :].bitcast(I32))
         offs_sb = load_list("offs_sb", offs)
-        table_words = keep.tile([P, T], U32, name="table_words", align_bytes=64)
-        nc.scalar.dma_start(
-            table_words[:].bitcast(I32), x_words[0].rearrange("p n t -> p (n t)").bitcast(I32)
-        )
-        w_rows = w1.rearrange("(p j) c -> p j c", j=PACK)
-        w_raw = []
-        for h, (start, width) in enumerate(W_PIECES):
-            raw = keep.tile([P, PACK, width], F32, name=f"w_raw{h}")
-            nc.scalar.dma_start(raw[:], w_rows[:, :, start : start + width])
-            w_raw.append(raw)
         ca_sb = load_list("ca_sb", ca)
         cb_sb = load_list("cb_sb", cb)
+        w_rows = w1.rearrange("(p j) c -> p j c", j=PACK)
+        w_raw = []
+        for h in range(2):
+            raw = keep.tile([P, PACK, HALF], F32, name=f"w_raw{h}")
+            nc.sync.dma_start(raw[:], w_rows[:, :, h * HALF : (h + 1) * HALF])
+            w_raw.append(raw)
+        table_words = keep.tile([P, T], U32, name="table_words", align_bytes=64)
+        nc.sync.dma_start(table_words[:].bitcast(I32), x_words[0].rearrange("p n t -> p (n t)").bitcast(I32))
         n2_sb = load_list("n2_sb", n2)
         n1_sb = load_list("n1_sb", n1)
         n4_sb = load_list("n4_sb", n4)
@@ -70,50 +68,48 @@ def tile_picked_ccmpmaxbsum_none_p_kernel(
         def gather_dealt(dst, table, offsets):
             nc.vector.tensor_copy(dst[:].rearrange("p (t m) -> p m t", t=PACK), table[:].indirect(offsets[:]))
 
-        tok_words = keep.tile([P, S], U32, name="tok_words", align_bytes=64)
-        nc.vector.tensor_copy(tok_words[:], table_words[:].indirect(offs_sb[:]))
         tok_scales = keep.tile([P, S], U8, name="tok_scales", align_bytes=64)
         nc.vector.tensor_copy(tok_scales[:], table_scales[:].indirect(offs_sb[:]))
-        a_words = keep.tile([P, C], U32, name="a_words", align_bytes=64)
-        gather_dealt(a_words, table_words, ca_sb)
+        a_scales = keep.tile([P, C], U8, name="a_scales", align_bytes=64)
+        gather_dealt(a_scales, table_scales, ca_sb)
+        b_scales = keep.tile([P, C], U8, name="b_scales", align_bytes=64)
+        gather_dealt(b_scales, table_scales, cb_sb)
 
-        w_bf = shared.tile([P, H * PACK], BF16, name="w_bf", align_bytes=64, offset=0)
+        w_bf = keep.tile([P, H * PACK], BF16, name="w_bf", align_bytes=64)
         w_bf_view = w_bf[:].rearrange("p (t m j) -> p m j t", t=PACK, j=PACK)
-        for h, (start, width) in enumerate(W_PIECES):
+        for h in range(2):
             nc.scalar.activation(
-                w_bf_view[:, start // PACK : (start + width) // PACK],
+                w_bf_view[:, h * HALF // PACK : (h + 1) * HALF // PACK],
                 w_raw[h][:].rearrange("p j (m t) -> p m j t", t=PACK),
                 COPY,
             )
         w_codes = keep.tile([P, H], U32, name="w_codes", align_bytes=64)
         w_scales = keep.tile([P, H], U8, name="w_scales", align_bytes=64)
-        for t in range(PACK):
-            rows = slice(t * P, (t + 1) * P)
-            nc.vector.quantize_mx(
-                out=w_codes[:, rows].bitcast(FP8X4), scales=w_scales[:, rows], in_=w_bf[:, t * H : (t + 1) * H]
-            )
+        nc.vector.quantize_mx(out=w_codes[:].bitcast(FP8X4), scales=w_scales[:], in_=w_bf[:])
 
         y_sb = [keep.tile([P, S], F32, name=f"y_sb{t}") for t in range(PACK)]
-        for t in range(PACK):
-            rows = slice(t * P, (t + 1) * P)
-            bank = psum.tile([P, S], F32, name=f"y_ps{t}", tag=f"bank{PACK + t}")
-            nc.tensor.matmul_mx(
-                bank[:],
-                lhsT=w_codes[:, rows].bitcast(FP8X4),
-                lhsT_scale=w_scales[:, rows],
-                rhs=tok_words[:].bitcast(FP8X4),
-                rhs_scale=tok_scales[:],
-                start=True,
-                stop=True,
-            )
-            nc.scalar.activation(y_sb[t][:], bank[:], COPY, scale=gs_sb[:, t : t + 1])
+        for h in range(2):
+            tok_words = keep.tile([P, HALF], U32, name=f"tok_words{h}", align_bytes=64)
+            nc.vector.tensor_copy(tok_words[:], table_words[:].indirect(entries(offs_sb, h * HALF, HALF)))
+            cols = slice(h * HALF, (h + 1) * HALF)
+            for t in range(PACK):
+                rows = slice(t * P, (t + 1) * P)
+                bank = psum.tile([P, S], F32, name=f"y_ps{h}{t}", tag=f"bank{PACK * h + t}")
+                nc.tensor.matmul_mx(
+                    bank[:, 0:HALF],
+                    lhsT=w_codes[:, rows].bitcast(FP8X4),
+                    lhsT_scale=w_scales[:, rows],
+                    rhs=tok_words[:].bitcast(FP8X4),
+                    rhs_scale=tok_scales[:, cols],
+                    start=True,
+                    stop=True,
+                )
+                nc.scalar.activation(y_sb[t][:, cols], bank[:, 0:HALF], COPY, scale=gs_sb[:, t : t + 1])
 
-        b_words = shared.tile([P, C], U32, name="b_words", align_bytes=64, offset=0)
+        a_words = keep.tile([P, C], U32, name="a_words", align_bytes=64)
+        gather_dealt(a_words, table_words, ca_sb)
+        b_words = keep.tile([P, C], U32, name="b_words", align_bytes=64)
         gather_dealt(b_words, table_words, cb_sb)
-        b_scales = shared.tile([P, C], U8, name="b_scales", align_bytes=64, offset=2048)
-        gather_dealt(b_scales, table_scales, cb_sb)
-        a_scales = shared.tile([P, C], U8, name="a_scales", align_bytes=64, offset=3072)
-        gather_dealt(a_scales, table_scales, ca_sb)
 
         a_ps = [psum.tile([P, S], F32, name=f"a_ps{t}", tag=f"bank{2 * t}") for t in range(PACK)]
         b_ps = [psum.tile([P, S], F32, name=f"b_ps{t}", tag=f"bank{2 * t + 1}") for t in range(PACK)]
@@ -152,26 +148,36 @@ def tile_picked_ccmpmaxbsum_none_p_kernel(
                         start=True,
                         stop=True,
                     )
-                    if piece + 1 < len(Z_PIECES):
+                    if piece + 1 < len(Z_PIECES) or held is b_sb[0]:
                         nc.scalar.activation(held[:, cols], bank[:, cols], COPY, scale=0.0625)
                     else:
                         nc.vector.tensor_scalar_mul(held[:, cols], bank[:, cols], 0.0625)
 
         out_rows = out.rearrange("(p t) j -> p t j", t=PACK)
         for t in range(PACK):
+            last = t == PACK - 1
             result = keep.tile([P, S], F32, name=f"result{t}")
-            for h in range(2):
-                cols = slice(h * HALF, (h + 1) * HALF)
+            for start, width in LAST_PIECES if last else OUT_PIECES:
+                cols = slice(start, start + width)
                 b_at = ring.tile([P, HALF], F32, name="b_at")
-                nc.scalar.activation(b_at[:], b_sb[t][:].indirect(entries(n4_sb, h * HALF, HALF)), COPY)
+                nc.scalar.activation(b_at[:, :width], b_sb[t][:].indirect(entries(n4_sb, start, width)), COPY)
                 a_at = ring.tile([P, HALF], F32, name="a_at")
-                nc.scalar.activation(a_at[:], a_sb[t][:].indirect(entries(n3_sb, h * HALF, HALF)), COPY)
+                a_window = a_sb[t][:].indirect(entries(n3_sb, start, width))
+                if last:
+                    nc.vector.tensor_copy(a_at[:, :width], a_window)
+                else:
+                    nc.scalar.activation(a_at[:, :width], a_window, COPY)
                 larger = ring.tile([P, HALF], F32, name="larger")
-                nc.vector.tensor_tensor(larger[:], a_sb[t][:, cols], b_at[:], ALU.max)
+                nc.vector.scalar_tensor_tensor(
+                    larger[:, :width], a_ps[t][:, cols], 0.0625, b_at[:, :width], ALU.mult, ALU.max
+                )
                 smaller = ring.tile([P, HALF], F32, name="smaller")
-                nc.vector.tensor_tensor(smaller[:], a_at[:], b_sb[t][:, cols], ALU.min)
-                nc.vector.tensor_tensor(result[:, cols], larger[:], smaller[:], ALU.subtract)
-                if t == PACK - 1:
+                nc.vector.scalar_tensor_tensor(
+                    smaller[:, :width], b_ps[t][:, cols], 0.0625, a_at[:, :width], ALU.mult, ALU.min
+                )
+                engine = nc.vector if last else nc.gpsimd
+                engine.tensor_tensor(result[:, cols], larger[:, :width], smaller[:, :width], ALU.subtract)
+                if last:
                     nc.sync.dma_start(out_rows[:, t, cols], result[:, cols])
-            if t < PACK - 1:
+            if not last:
                 nc.sync.dma_start(out_rows[:, t, :], result[:])

@@ -20,7 +20,10 @@ PACK = 4
 HALF = 256
 OUT_PIECES = ((0, 256), (256, 256))
 LAST_PIECES = ((0, 256), (256, 128), (384, 128))
-Z_PIECES = ((0, 256), (256, 256))
+Z_PIECES = ((0, 256), (256, 128), (384, 128))
+Z_AT = (128, 0, 512)
+RUN = 8
+A_ON_VECTOR = ((3, 0), (3, 256), (2, 256))
 
 
 def entries(offsets, start, count):
@@ -66,7 +69,7 @@ def tile_picked_ccmpmaxbsum_none_p_kernel(
         n3_sb = load_list("n3_sb", n3)
 
         def gather_dealt(dst, table, offsets):
-            nc.vector.tensor_copy(dst[:].rearrange("p (t m) -> p m t", t=PACK), table[:].indirect(offsets[:]))
+            nc.vector.tensor_copy(dst[:].rearrange("p (t g b) -> p g t b", t=PACK, b=RUN), table[:].indirect(offsets[:]))
 
         tok_scales = keep.tile([P, S], U8, name="tok_scales", align_bytes=64)
         nc.vector.tensor_copy(tok_scales[:], table_scales[:].indirect(offs_sb[:]))
@@ -87,29 +90,56 @@ def tile_picked_ccmpmaxbsum_none_p_kernel(
         w_scales = keep.tile([P, H], U8, name="w_scales", align_bytes=64)
         nc.vector.quantize_mx(out=w_codes[:].bitcast(FP8X4), scales=w_scales[:], in_=w_bf[:])
 
-        y_sb = [keep.tile([P, S], F32, name=f"y_sb{t}") for t in range(PACK)]
+        tok_words = []
         for h in range(2):
-            tok_words = keep.tile([P, HALF], U32, name=f"tok_words{h}", align_bytes=64)
-            nc.vector.tensor_copy(tok_words[:], table_words[:].indirect(entries(offs_sb, h * HALF, HALF)))
-            cols = slice(h * HALF, (h + 1) * HALF)
-            for t in range(PACK):
-                rows = slice(t * P, (t + 1) * P)
-                bank = psum.tile([P, S], F32, name=f"y_ps{h}{t}", tag=f"bank{PACK * h + t}")
-                nc.tensor.matmul_mx(
-                    bank[:, 0:HALF],
-                    lhsT=w_codes[:, rows].bitcast(FP8X4),
-                    lhsT_scale=w_scales[:, rows],
-                    rhs=tok_words[:].bitcast(FP8X4),
-                    rhs_scale=tok_scales[:, cols],
-                    start=True,
-                    stop=True,
-                )
-                nc.scalar.activation(y_sb[t][:, cols], bank[:, 0:HALF], COPY, scale=gs_sb[:, t : t + 1])
-
+            words = keep.tile([P, HALF], U32, name=f"tok_words{h}", align_bytes=64)
+            nc.vector.tensor_copy(words[:], table_words[:].indirect(entries(offs_sb, h * HALF, HALF)))
+            tok_words.append(words)
         a_words = keep.tile([P, C], U32, name="a_words", align_bytes=64)
         gather_dealt(a_words, table_words, ca_sb)
         b_words = keep.tile([P, C], U32, name="b_words", align_bytes=64)
         gather_dealt(b_words, table_words, cb_sb)
+
+        y_sb = [keep.tile([P, S], F32, name=f"y_sb{t}") for t in range(PACK)]
+
+        def project(h, t):
+            rows = slice(t * P, (t + 1) * P)
+            cols = slice(h * HALF, (h + 1) * HALF)
+            bank = psum.tile([P, S], F32, name=f"y_ps{h}{t}", tag=f"bank{PACK * h + t}")
+            nc.tensor.matmul_mx(
+                bank[:, 0:HALF],
+                lhsT=w_codes[:, rows].bitcast(FP8X4),
+                lhsT_scale=w_scales[:, rows],
+                rhs=tok_words[h][:].bitcast(FP8X4),
+                rhs_scale=tok_scales[:, cols],
+                start=True,
+                stop=True,
+            )
+            if h == 0 or t == 0:
+                nc.scalar.activation(y_sb[t][:, cols], bank[:, 0:HALF], COPY, scale=gs_sb[:, t : t + 1])
+            else:
+                nc.vector.tensor_scalar_mul(y_sb[t][:, cols], bank[:, 0:HALF], gs_sb[:, t : t + 1])
+
+        z_room = keep.tile([P, 1152], F32, name="z_room")
+        z_f32 = [
+            z_room[:, at : at + PACK * width].rearrange("p (t c) -> p t c", t=PACK)
+            for at, (start, width) in zip(Z_AT, Z_PIECES)
+        ]
+
+        def mix(piece, t):
+            start, width = Z_PIECES[piece]
+            second = keep.tile([P, width], F32, name=f"second{piece}{t}")
+            nc.scalar.activation(second[:], y_sb[t][:].indirect(entries(n2_sb, start, width)), COPY, scale=0.75)
+            nc.vector.tensor_tensor(
+                z_f32[piece][:, t, :], y_sb[t][:].indirect(entries(n1_sb, start, width)), second[:], ALU.add
+            )
+
+        for t in range(PACK):
+            project(0, t)
+        for t in range(PACK):
+            project(1, t)
+        for t in range(PACK):
+            mix(0, t)
 
         a_ps = [psum.tile([P, S], F32, name=f"a_ps{t}", tag=f"bank{2 * t}") for t in range(PACK)]
         b_ps = [psum.tile([P, S], F32, name=f"b_ps{t}", tag=f"bank{2 * t + 1}") for t in range(PACK)]
@@ -118,17 +148,13 @@ def tile_picked_ccmpmaxbsum_none_p_kernel(
 
         for piece, (start, width) in enumerate(Z_PIECES):
             cols = slice(start, start + width)
-            z_f32 = keep.tile([P, PACK, width], F32, name=f"z_f32_{piece}")
-            for t in range(PACK):
-                second = keep.tile([P, width], F32, name=f"second{piece}{t}")
-                nc.scalar.activation(second[:], y_sb[t][:].indirect(entries(n2_sb, start, width)), COPY, scale=0.75)
-                nc.vector.tensor_tensor(
-                    z_f32[:, t, :], y_sb[t][:].indirect(entries(n1_sb, start, width)), second[:], ALU.add
-                )
+            if piece > 0:
+                for t in range(PACK):
+                    mix(piece, t)
             z_bf = keep.tile([P, width * PACK], BF16, name=f"z_bf{piece}", align_bytes=64)
             nc.vector.tensor_copy(
                 z_bf[:].rearrange("p (c i t) -> p c t i", i=4, t=PACK),
-                z_f32[:].rearrange("p t (c i) -> p c t i", i=4),
+                z_f32[piece].rearrange("p t (c i) -> p c t i", i=4),
             )
             z_codes = keep.tile([P, width], U32, name=f"z_codes{piece}", align_bytes=64)
             z_scales = keep.tile([P, width], U8, name=f"z_scales{piece}", align_bytes=64)
@@ -148,36 +174,44 @@ def tile_picked_ccmpmaxbsum_none_p_kernel(
                         start=True,
                         stop=True,
                     )
-                    if piece + 1 < len(Z_PIECES) or held is b_sb[0]:
+                    if piece == 0:
                         nc.scalar.activation(held[:, cols], bank[:, cols], COPY, scale=0.0625)
-                    else:
-                        nc.vector.tensor_scalar_mul(held[:, cols], bank[:, cols], 0.0625)
 
-        out_rows = out.rearrange("(p t) j -> p t j", t=PACK)
+        upper = slice(HALF, S)
+        nc.scalar.activation(b_sb[0][:, upper], b_ps[0][:, upper], COPY, scale=0.0625)
+        for t in range(PACK):
+            if t > 0:
+                nc.vector.tensor_scalar_mul(b_sb[t][:, upper], b_ps[t][:, upper], 0.0625)
+            nc.vector.tensor_scalar_mul(a_sb[t][:, upper], a_ps[t][:, upper], 0.0625)
+
+        a_at = [keep.tile([P, S], F32, name=f"a_at{t}") for t in range(PACK)]
+        b_at = [keep.tile([P, S], F32, name=f"b_at{t}") for t in range(PACK)]
+        for t, start in A_ON_VECTOR:
+            nc.vector.tensor_copy(a_at[t][:, start : start + HALF], a_sb[t][:].indirect(entries(n3_sb, start, HALF)))
+
+        out_rows = out.rearrange("(g t b) j -> t g b j", t=PACK, b=RUN)
         for t in range(PACK):
             last = t == PACK - 1
             result = keep.tile([P, S], F32, name=f"result{t}")
+            smaller = ring.tile([P, S], F32, name="smaller")
+            larger = ring.tile([P, S], F32, name="larger")
+            if last:
+                nc.vector.scalar_tensor_tensor(smaller[:], b_ps[t][:], 0.0625, a_at[t][:], ALU.mult, ALU.min)
             for start, width in LAST_PIECES if last else OUT_PIECES:
                 cols = slice(start, start + width)
-                b_at = ring.tile([P, HALF], F32, name="b_at")
-                nc.scalar.activation(b_at[:, :width], b_sb[t][:].indirect(entries(n4_sb, start, width)), COPY)
-                a_at = ring.tile([P, HALF], F32, name="a_at")
-                a_window = a_sb[t][:].indirect(entries(n3_sb, start, width))
-                if last:
-                    nc.vector.tensor_copy(a_at[:, :width], a_window)
-                else:
-                    nc.scalar.activation(a_at[:, :width], a_window, COPY)
-                larger = ring.tile([P, HALF], F32, name="larger")
+                nc.scalar.activation(b_at[t][:, cols], b_sb[t][:].indirect(entries(n4_sb, start, width)), COPY)
+                if (t, start) not in A_ON_VECTOR and not last:
+                    nc.scalar.activation(a_at[t][:, cols], a_sb[t][:].indirect(entries(n3_sb, start, width)), COPY)
                 nc.vector.scalar_tensor_tensor(
-                    larger[:, :width], a_ps[t][:, cols], 0.0625, b_at[:, :width], ALU.mult, ALU.max
+                    larger[:, cols], a_ps[t][:, cols], 0.0625, b_at[t][:, cols], ALU.mult, ALU.max
                 )
-                smaller = ring.tile([P, HALF], F32, name="smaller")
-                nc.vector.scalar_tensor_tensor(
-                    smaller[:, :width], b_ps[t][:, cols], 0.0625, a_at[:, :width], ALU.mult, ALU.min
-                )
+                if not last:
+                    nc.vector.scalar_tensor_tensor(
+                        smaller[:, cols], b_ps[t][:, cols], 0.0625, a_at[t][:, cols], ALU.mult, ALU.min
+                    )
                 engine = nc.vector if last else nc.gpsimd
-                engine.tensor_tensor(result[:, cols], larger[:, :width], smaller[:, :width], ALU.subtract)
-                if last:
-                    nc.sync.dma_start(out_rows[:, t, cols], result[:, cols])
-            if not last:
-                nc.sync.dma_start(out_rows[:, t, :], result[:])
+                engine.tensor_tensor(result[:, cols], larger[:, cols], smaller[:, cols], ALU.subtract)
+                if t >= 2:
+                    nc.sync.dma_start(out_rows[t][:, :, cols], result[:, cols])
+            if t < 2:
+                nc.sync.dma_start(out_rows[t], result[:])

@@ -23,7 +23,7 @@ LAST_PIECES = ((0, 256), (256, 128), (384, 128))
 Z_PIECES = ((0, 256), (256, 128), (384, 128))
 Z_AT = (128, 0, 512)
 RUN = 8
-A_ON_VECTOR = ((3, 0), (3, 256), (2, 256))
+A_ON_VECTOR = ((3, 0), (3, 256))
 
 
 def entries(offsets, start, count):
@@ -36,6 +36,7 @@ def tile_picked_ccmpmaxbsum_none_p_kernel(
     nc = tc.nc
     with ExitStack() as ctx:
         keep = ctx.enter_context(tc.tile_pool(name="keep", bufs=1))
+        shared = ctx.enter_context(tc.tile_pool(name="shared", bufs=1))
         ring = ctx.enter_context(tc.tile_pool(name="ring", bufs=4))
         psum = ctx.enter_context(tc.psum_pool(name="psum", bufs=1))
 
@@ -55,30 +56,32 @@ def tile_picked_ccmpmaxbsum_none_p_kernel(
         offs_sb = load_list("offs_sb", offs)
         ca_sb = load_list("ca_sb", ca)
         cb_sb = load_list("cb_sb", cb)
+        table_words = keep.tile([P, T], U32, name="table_words", align_bytes=64)
+        nc.sync.dma_start(table_words[:].bitcast(I32), x_words[0].rearrange("p n t -> p (n t)").bitcast(I32))
         w_rows = w1.rearrange("(p j) c -> p j c", j=PACK)
         w_raw = []
         for h in range(2):
             raw = keep.tile([P, PACK, HALF], F32, name=f"w_raw{h}")
             nc.sync.dma_start(raw[:], w_rows[:, :, h * HALF : (h + 1) * HALF])
             w_raw.append(raw)
-        table_words = keep.tile([P, T], U32, name="table_words", align_bytes=64)
-        nc.sync.dma_start(table_words[:].bitcast(I32), x_words[0].rearrange("p n t -> p (n t)").bitcast(I32))
         n2_sb = load_list("n2_sb", n2)
         n1_sb = load_list("n1_sb", n1)
         n4_sb = load_list("n4_sb", n4)
         n3_sb = load_list("n3_sb", n3)
 
         def gather_dealt(dst, table, offsets):
-            nc.vector.tensor_copy(dst[:].rearrange("p (t g b) -> p g t b", t=PACK, b=RUN), table[:].indirect(offsets[:]))
+            nc.vector.tensor_copy(
+                dst[:].rearrange("p (t g b) -> p g t b", t=PACK, b=RUN), table[:].indirect(offsets[:])
+            )
 
+        tok_words = keep.tile([P, S], U32, name="tok_words", align_bytes=64)
+        nc.vector.tensor_copy(tok_words[:], table_words[:].indirect(offs_sb[:]))
         tok_scales = keep.tile([P, S], U8, name="tok_scales", align_bytes=64)
         nc.vector.tensor_copy(tok_scales[:], table_scales[:].indirect(offs_sb[:]))
-        a_scales = keep.tile([P, C], U8, name="a_scales", align_bytes=64)
-        gather_dealt(a_scales, table_scales, ca_sb)
-        b_scales = keep.tile([P, C], U8, name="b_scales", align_bytes=64)
-        gather_dealt(b_scales, table_scales, cb_sb)
+        a_words = keep.tile([P, C], U32, name="a_words", align_bytes=64)
+        gather_dealt(a_words, table_words, ca_sb)
 
-        w_bf = keep.tile([P, H * PACK], BF16, name="w_bf", align_bytes=64)
+        w_bf = shared.tile([P, H * PACK], BF16, name="w_bf", align_bytes=64, offset=0)
         w_bf_view = w_bf[:].rearrange("p (t m j) -> p m j t", t=PACK, j=PACK)
         for h in range(2):
             nc.scalar.activation(
@@ -88,37 +91,37 @@ def tile_picked_ccmpmaxbsum_none_p_kernel(
             )
         w_codes = keep.tile([P, H], U32, name="w_codes", align_bytes=64)
         w_scales = keep.tile([P, H], U8, name="w_scales", align_bytes=64)
-        nc.vector.quantize_mx(out=w_codes[:].bitcast(FP8X4), scales=w_scales[:], in_=w_bf[:])
+        for t in range(PACK):
+            rows = slice(t * P, (t + 1) * P)
+            nc.vector.quantize_mx(
+                out=w_codes[:, rows].bitcast(FP8X4), scales=w_scales[:, rows], in_=w_bf[:, t * H : (t + 1) * H]
+            )
 
-        tok_words = []
-        for h in range(2):
-            words = keep.tile([P, HALF], U32, name=f"tok_words{h}", align_bytes=64)
-            nc.vector.tensor_copy(words[:], table_words[:].indirect(entries(offs_sb, h * HALF, HALF)))
-            tok_words.append(words)
-        a_words = keep.tile([P, C], U32, name="a_words", align_bytes=64)
-        gather_dealt(a_words, table_words, ca_sb)
-        b_words = keep.tile([P, C], U32, name="b_words", align_bytes=64)
+        b_words = shared.tile([P, C], U32, name="b_words", align_bytes=64, offset=0)
         gather_dealt(b_words, table_words, cb_sb)
+        b_scales = shared.tile([P, C], U8, name="b_scales", align_bytes=64, offset=2048)
+        gather_dealt(b_scales, table_scales, cb_sb)
+        a_scales = shared.tile([P, C], U8, name="a_scales", align_bytes=64, offset=3072)
+        gather_dealt(a_scales, table_scales, ca_sb)
 
         y_sb = [keep.tile([P, S], F32, name=f"y_sb{t}") for t in range(PACK)]
 
-        def project(h, t):
+        def project(t):
             rows = slice(t * P, (t + 1) * P)
-            cols = slice(h * HALF, (h + 1) * HALF)
-            bank = psum.tile([P, S], F32, name=f"y_ps{h}{t}", tag=f"bank{PACK * h + t}")
+            bank = psum.tile([P, S], F32, name=f"y_ps{t}", tag=f"bank{PACK + t}")
             nc.tensor.matmul_mx(
-                bank[:, 0:HALF],
+                bank[:],
                 lhsT=w_codes[:, rows].bitcast(FP8X4),
                 lhsT_scale=w_scales[:, rows],
-                rhs=tok_words[h][:].bitcast(FP8X4),
-                rhs_scale=tok_scales[:, cols],
+                rhs=tok_words[:].bitcast(FP8X4),
+                rhs_scale=tok_scales[:],
                 start=True,
                 stop=True,
             )
-            if h == 0 or t == 0:
-                nc.scalar.activation(y_sb[t][:, cols], bank[:, 0:HALF], COPY, scale=gs_sb[:, t : t + 1])
+            if t < PACK - 1:
+                nc.scalar.activation(y_sb[t][:], bank[:], COPY, scale=gs_sb[:, t : t + 1])
             else:
-                nc.vector.tensor_scalar_mul(y_sb[t][:, cols], bank[:, 0:HALF], gs_sb[:, t : t + 1])
+                nc.vector.tensor_scalar_mul(y_sb[t][:], bank[:], gs_sb[:, t : t + 1])
 
         z_room = keep.tile([P, 1152], F32, name="z_room")
         z_f32 = [
@@ -135,10 +138,7 @@ def tile_picked_ccmpmaxbsum_none_p_kernel(
             )
 
         for t in range(PACK):
-            project(0, t)
-        for t in range(PACK):
-            project(1, t)
-        for t in range(PACK):
+            project(t)
             mix(0, t)
 
         a_ps = [psum.tile([P, S], F32, name=f"a_ps{t}", tag=f"bank{2 * t}") for t in range(PACK)]
@@ -146,43 +146,54 @@ def tile_picked_ccmpmaxbsum_none_p_kernel(
         a_sb = [keep.tile([P, S], F32, name=f"a_sb{t}") for t in range(PACK)]
         b_sb = [keep.tile([P, S], F32, name=f"b_sb{t}") for t in range(PACK)]
 
-        for piece, (start, width) in enumerate(Z_PIECES):
-            cols = slice(start, start + width)
-            if piece > 0:
-                for t in range(PACK):
-                    mix(piece, t)
+        z_codes = [keep.tile([P, HALF], U32, name=f"z_codes{h}", align_bytes=64) for h in range(2)]
+        z_scales = [keep.tile([P, HALF], U8, name=f"z_scales{h}", align_bytes=64) for h in range(2)]
+
+        def quantise(piece):
+            start, width = Z_PIECES[piece]
             z_bf = keep.tile([P, width * PACK], BF16, name=f"z_bf{piece}", align_bytes=64)
             nc.vector.tensor_copy(
                 z_bf[:].rearrange("p (c i t) -> p c t i", i=4, t=PACK),
                 z_f32[piece].rearrange("p t (c i) -> p c t i", i=4),
             )
-            z_codes = keep.tile([P, width], U32, name=f"z_codes{piece}", align_bytes=64)
-            z_scales = keep.tile([P, width], U8, name=f"z_scales{piece}", align_bytes=64)
-            nc.vector.quantize_mx(out=z_codes[:].bitcast(FP8X4), scales=z_scales[:], in_=z_bf[:])
-            for t in range(PACK):
-                rows = slice(t * P, (t + 1) * P)
-                for words, scales, bank, held in (
-                    (b_words, b_scales, b_ps[t], b_sb[t]),
-                    (a_words, a_scales, a_ps[t], a_sb[t]),
-                ):
-                    nc.tensor.matmul_mx(
-                        bank[:, cols],
-                        lhsT=words[:, rows].bitcast(FP8X4),
-                        lhsT_scale=scales[:, rows],
-                        rhs=z_codes[:].bitcast(FP8X4),
-                        rhs_scale=z_scales[:],
-                        start=True,
-                        stop=True,
-                    )
-                    if piece == 0:
-                        nc.scalar.activation(held[:, cols], bank[:, cols], COPY, scale=0.0625)
+            h, within = divmod(start, HALF)
+            cols = slice(within, within + width)
+            nc.vector.quantize_mx(out=z_codes[h][:, cols].bitcast(FP8X4), scales=z_scales[h][:, cols], in_=z_bf[:])
 
-        upper = slice(HALF, S)
-        nc.scalar.activation(b_sb[0][:, upper], b_ps[0][:, upper], COPY, scale=0.0625)
+        def score(h, t, words, scales, bank):
+            rows = slice(t * P, (t + 1) * P)
+            nc.tensor.matmul_mx(
+                bank[:, h * HALF : (h + 1) * HALF],
+                lhsT=words[:, rows].bitcast(FP8X4),
+                lhsT_scale=scales[:, rows],
+                rhs=z_codes[h][:].bitcast(FP8X4),
+                rhs_scale=z_scales[h][:],
+                start=True,
+                stop=True,
+            )
+
+        def empty(h, bank, held, on_scalar):
+            cols = slice(h * HALF, (h + 1) * HALF)
+            if on_scalar:
+                nc.scalar.activation(held[:, cols], bank[:, cols], COPY, scale=0.0625)
+            else:
+                nc.vector.tensor_scalar_mul(held[:, cols], bank[:, cols], 0.0625)
+
+        quantise(0)
         for t in range(PACK):
-            if t > 0:
-                nc.vector.tensor_scalar_mul(b_sb[t][:, upper], b_ps[t][:, upper], 0.0625)
-            nc.vector.tensor_scalar_mul(a_sb[t][:, upper], a_ps[t][:, upper], 0.0625)
+            score(0, t, b_words, b_scales, b_ps[t])
+            score(0, t, a_words, a_scales, a_ps[t])
+            empty(0, b_ps[t], b_sb[t], True)
+            empty(0, a_ps[t], a_sb[t], True)
+        for piece in (1, 2):
+            for t in range(PACK):
+                mix(piece, t)
+            quantise(piece)
+        for t in range(PACK):
+            score(1, t, b_words, b_scales, b_ps[t])
+            empty(1, b_ps[t], b_sb[t], t == 0)
+            score(1, t, a_words, a_scales, a_ps[t])
+            empty(1, a_ps[t], a_sb[t], False)
 
         a_at = [keep.tile([P, S], F32, name=f"a_at{t}") for t in range(PACK)]
         b_at = [keep.tile([P, S], F32, name=f"b_at{t}") for t in range(PACK)]
@@ -191,27 +202,53 @@ def tile_picked_ccmpmaxbsum_none_p_kernel(
 
         out_rows = out.rearrange("(g t b) j -> t g b j", t=PACK, b=RUN)
         for t in range(PACK):
-            last = t == PACK - 1
             result = keep.tile([P, S], F32, name=f"result{t}")
             smaller = ring.tile([P, S], F32, name="smaller")
             larger = ring.tile([P, S], F32, name="larger")
-            if last:
-                nc.vector.scalar_tensor_tensor(smaller[:], b_ps[t][:], 0.0625, a_at[t][:], ALU.mult, ALU.min)
-            for start, width in LAST_PIECES if last else OUT_PIECES:
-                cols = slice(start, start + width)
-                nc.scalar.activation(b_at[t][:, cols], b_sb[t][:].indirect(entries(n4_sb, start, width)), COPY)
-                if (t, start) not in A_ON_VECTOR and not last:
-                    nc.scalar.activation(a_at[t][:, cols], a_sb[t][:].indirect(entries(n3_sb, start, width)), COPY)
+
+            def fetch_b(start, width):
+                window = b_sb[t][:].indirect(entries(n4_sb, start, width))
+                nc.scalar.activation(b_at[t][:, start : start + width], window, COPY)
+
+            def fetch_a(start, width):
+                window = a_sb[t][:].indirect(entries(n3_sb, start, width))
+                nc.scalar.activation(a_at[t][:, start : start + width], window, COPY)
+
+            def take_larger(cols):
                 nc.vector.scalar_tensor_tensor(
                     larger[:, cols], a_ps[t][:, cols], 0.0625, b_at[t][:, cols], ALU.mult, ALU.max
                 )
-                if not last:
-                    nc.vector.scalar_tensor_tensor(
-                        smaller[:, cols], b_ps[t][:, cols], 0.0625, a_at[t][:, cols], ALU.mult, ALU.min
-                    )
-                engine = nc.vector if last else nc.gpsimd
+
+            def take_smaller(cols):
+                nc.vector.scalar_tensor_tensor(
+                    smaller[:, cols], b_ps[t][:, cols], 0.0625, a_at[t][:, cols], ALU.mult, ALU.min
+                )
+
+            def finish(cols, engine):
                 engine.tensor_tensor(result[:, cols], larger[:, cols], smaller[:, cols], ALU.subtract)
-                if t >= 2:
-                    nc.sync.dma_start(out_rows[t][:, :, cols], result[:, cols])
+                nc.sync.dma_start(out_rows[t][:, :, cols], result[:, cols])
+
+            whole = slice(0, S)
             if t < 2:
-                nc.sync.dma_start(out_rows[t], result[:])
+                for start, width in OUT_PIECES:
+                    fetch_b(start, width)
+                for start, width in OUT_PIECES:
+                    fetch_a(start, width)
+                take_larger(whole)
+                take_smaller(whole)
+                finish(whole, nc.gpsimd)
+            elif t == 2:
+                for start, width in OUT_PIECES:
+                    cols = slice(start, start + width)
+                    fetch_b(start, width)
+                    fetch_a(start, width)
+                    take_larger(cols)
+                    take_smaller(cols)
+                    finish(cols, nc.gpsimd if start == 0 else nc.vector)
+            else:
+                take_smaller(whole)
+                for start, width in LAST_PIECES:
+                    cols = slice(start, start + width)
+                    fetch_b(start, width)
+                    take_larger(cols)
+                    finish(cols, nc.vector)

@@ -2,7 +2,7 @@ from contextlib import ExitStack
 
 import concourse.mybir as mybir
 
-K, T, S, H, C = 512, 2048, 512, 512, 512
+T, S, H, C = 2048, 512, 512, 512
 FLOPS = 3 * 2 * 512 * 512 * 512
 
 F32 = mybir.dt.float32
@@ -17,13 +17,14 @@ COPY = mybir.ActivationFunctionType.Copy
 
 P = 128
 PACK = 4
-HALF = 256
-OUT_PIECES = ((0, 256), (256, 256))
-LAST_PIECES = ((0, 256), (256, 128), (384, 128))
-Z_PIECES = ((0, 256), (256, 128), (384, 128))
-Z_AT = (128, 0, 512)
-RUN = 8
-A_ON_VECTOR = ((3, 0), (3, 256))
+LAST = PACK - 1
+HALF = S // 2
+HALVES = ((0, HALF), (HALF, HALF))
+LAST_PIECES = ((0, HALF), (HALF, HALF // 2), (HALF + HALF // 2, HALF // 2))
+LINE = 4
+SHARED_TILE = 1
+SECOND_WEIGHT = 0.75
+SCORE_SCALE = 0.0625
 
 
 def entries(offsets, start, count):
@@ -36,8 +37,7 @@ def tile_picked_ccmpmaxbsum_none_p_kernel(
     nc = tc.nc
     with ExitStack() as ctx:
         keep = ctx.enter_context(tc.tile_pool(name="keep", bufs=1))
-        shared = ctx.enter_context(tc.tile_pool(name="shared", bufs=1))
-        ring = ctx.enter_context(tc.tile_pool(name="ring", bufs=4))
+        ring = ctx.enter_context(tc.tile_pool(name="ring", bufs=PACK))
         psum = ctx.enter_context(tc.psum_pool(name="psum", bufs=1))
 
         def load_list(name, src):
@@ -56,32 +56,30 @@ def tile_picked_ccmpmaxbsum_none_p_kernel(
         offs_sb = load_list("offs_sb", offs)
         ca_sb = load_list("ca_sb", ca)
         cb_sb = load_list("cb_sb", cb)
-        table_words = keep.tile([P, T], U32, name="table_words", align_bytes=64)
-        nc.sync.dma_start(table_words[:].bitcast(I32), x_words[0].rearrange("p n t -> p (n t)").bitcast(I32))
         w_rows = w1.rearrange("(p j) c -> p j c", j=PACK)
         w_raw = []
         for h in range(2):
             raw = keep.tile([P, PACK, HALF], F32, name=f"w_raw{h}")
             nc.sync.dma_start(raw[:], w_rows[:, :, h * HALF : (h + 1) * HALF])
             w_raw.append(raw)
+        table_words = keep.tile([P, T], U32, name="table_words", align_bytes=64)
+        nc.sync.dma_start(table_words[:].bitcast(I32), x_words[0].rearrange("p n t -> p (n t)").bitcast(I32))
         n2_sb = load_list("n2_sb", n2)
         n1_sb = load_list("n1_sb", n1)
         n4_sb = load_list("n4_sb", n4)
         n3_sb = load_list("n3_sb", n3)
 
         def gather_dealt(dst, table, offsets):
-            nc.vector.tensor_copy(
-                dst[:].rearrange("p (t g b) -> p g t b", t=PACK, b=RUN), table[:].indirect(offsets[:])
-            )
+            nc.vector.tensor_copy(dst[:].rearrange("p (t m) -> p m t", t=PACK), table[:].indirect(offsets[:]))
 
-        tok_words = keep.tile([P, S], U32, name="tok_words", align_bytes=64)
-        nc.vector.tensor_copy(tok_words[:], table_words[:].indirect(offs_sb[:]))
         tok_scales = keep.tile([P, S], U8, name="tok_scales", align_bytes=64)
         nc.vector.tensor_copy(tok_scales[:], table_scales[:].indirect(offs_sb[:]))
-        a_words = keep.tile([P, C], U32, name="a_words", align_bytes=64)
-        gather_dealt(a_words, table_words, ca_sb)
+        a_scales = keep.tile([P, C], U8, name="a_scales", align_bytes=64)
+        gather_dealt(a_scales, table_scales, ca_sb)
+        b_scales = keep.tile([P, C], U8, name="b_scales", align_bytes=64)
+        gather_dealt(b_scales, table_scales, cb_sb)
 
-        w_bf = shared.tile([P, H * PACK], BF16, name="w_bf", align_bytes=64, offset=0)
+        w_bf = keep.tile([P, H * PACK], BF16, name="w_bf", align_bytes=64)
         w_bf_view = w_bf[:].rearrange("p (t m j) -> p m j t", t=PACK, j=PACK)
         for h in range(2):
             nc.scalar.activation(
@@ -91,54 +89,54 @@ def tile_picked_ccmpmaxbsum_none_p_kernel(
             )
         w_codes = keep.tile([P, H], U32, name="w_codes", align_bytes=64)
         w_scales = keep.tile([P, H], U8, name="w_scales", align_bytes=64)
-        for t in range(PACK):
-            rows = slice(t * P, (t + 1) * P)
-            nc.vector.quantize_mx(
-                out=w_codes[:, rows].bitcast(FP8X4), scales=w_scales[:, rows], in_=w_bf[:, t * H : (t + 1) * H]
-            )
+        nc.vector.quantize_mx(out=w_codes[:].bitcast(FP8X4), scales=w_scales[:], in_=w_bf[:])
 
-        b_words = shared.tile([P, C], U32, name="b_words", align_bytes=64, offset=0)
+        tok_words = []
+        for h in range(2):
+            words = keep.tile([P, HALF], U32, name=f"tok_words{h}", align_bytes=64)
+            nc.vector.tensor_copy(words[:], table_words[:].indirect(entries(offs_sb, h * HALF, HALF)))
+            tok_words.append(words)
+        a_words = keep.tile([P, C], U32, name="a_words", align_bytes=64)
+        gather_dealt(a_words, table_words, ca_sb)
+        b_words = keep.tile([P, C], U32, name="b_words", align_bytes=64)
         gather_dealt(b_words, table_words, cb_sb)
-        b_scales = shared.tile([P, C], U8, name="b_scales", align_bytes=64, offset=2048)
-        gather_dealt(b_scales, table_scales, cb_sb)
-        a_scales = shared.tile([P, C], U8, name="a_scales", align_bytes=64, offset=3072)
-        gather_dealt(a_scales, table_scales, ca_sb)
 
         y_sb = [keep.tile([P, S], F32, name=f"y_sb{t}") for t in range(PACK)]
 
-        def project(t):
+        def project(h, t):
             rows = slice(t * P, (t + 1) * P)
-            bank = psum.tile([P, S], F32, name=f"y_ps{t}", tag=f"bank{PACK + t}")
+            cols = slice(h * HALF, (h + 1) * HALF)
+            bank = psum.tile([P, S], F32, name=f"y_ps{h}{t}", tag=f"bank{PACK * h + t}")
             nc.tensor.matmul_mx(
-                bank[:],
+                bank[:, 0:HALF],
                 lhsT=w_codes[:, rows].bitcast(FP8X4),
                 lhsT_scale=w_scales[:, rows],
-                rhs=tok_words[:].bitcast(FP8X4),
-                rhs_scale=tok_scales[:],
+                rhs=tok_words[h][:].bitcast(FP8X4),
+                rhs_scale=tok_scales[:, cols],
                 start=True,
                 stop=True,
             )
-            if t < PACK - 1:
-                nc.scalar.activation(y_sb[t][:], bank[:], COPY, scale=gs_sb[:, t : t + 1])
+            if (h, t) != (1, LAST):
+                nc.scalar.activation(y_sb[t][:, cols], bank[:, 0:HALF], COPY, scale=gs_sb[:, t : t + 1])
             else:
-                nc.vector.tensor_scalar_mul(y_sb[t][:], bank[:], gs_sb[:, t : t + 1])
+                nc.vector.tensor_scalar_mul(y_sb[t][:, cols], bank[:, 0:HALF], gs_sb[:, t : t + 1])
 
-        z_room = keep.tile([P, 1152], F32, name="z_room")
-        z_f32 = [
-            z_room[:, at : at + PACK * width].rearrange("p (t c) -> p t c", t=PACK)
-            for at, (start, width) in zip(Z_AT, Z_PIECES)
-        ]
+        z_room = keep.tile([P, (PACK + 1) * HALF], F32, name="z_room")
+        z_f32 = [z_room[:, at : at + PACK * HALF].rearrange("p (t c) -> p t c", t=PACK) for at in (HALF, 0)]
 
-        def mix(piece, t):
-            start, width = Z_PIECES[piece]
-            second = keep.tile([P, width], F32, name=f"second{piece}{t}")
-            nc.scalar.activation(second[:], y_sb[t][:].indirect(entries(n2_sb, start, width)), COPY, scale=0.75)
+        def mix(h, t):
+            second = keep.tile([P, HALF], F32, name=f"second{h}{t}")
+            nc.scalar.activation(
+                second[:], y_sb[t][:].indirect(entries(n2_sb, h * HALF, HALF)), COPY, scale=SECOND_WEIGHT
+            )
             nc.vector.tensor_tensor(
-                z_f32[piece][:, t, :], y_sb[t][:].indirect(entries(n1_sb, start, width)), second[:], ALU.add
+                z_f32[h][:, t, :], y_sb[t][:].indirect(entries(n1_sb, h * HALF, HALF)), second[:], ALU.add
             )
 
         for t in range(PACK):
-            project(t)
+            project(0, t)
+        for t in range(PACK):
+            project(1, t)
             mix(0, t)
 
         a_ps = [psum.tile([P, S], F32, name=f"a_ps{t}", tag=f"bank{2 * t}") for t in range(PACK)]
@@ -149,16 +147,13 @@ def tile_picked_ccmpmaxbsum_none_p_kernel(
         z_codes = [keep.tile([P, HALF], U32, name=f"z_codes{h}", align_bytes=64) for h in range(2)]
         z_scales = [keep.tile([P, HALF], U8, name=f"z_scales{h}", align_bytes=64) for h in range(2)]
 
-        def quantise(piece):
-            start, width = Z_PIECES[piece]
-            z_bf = keep.tile([P, width * PACK], BF16, name=f"z_bf{piece}", align_bytes=64)
+        def quantise(h):
+            z_bf = keep.tile([P, HALF * PACK], BF16, name=f"z_bf{h}", align_bytes=64)
             nc.vector.tensor_copy(
-                z_bf[:].rearrange("p (c i t) -> p c t i", i=4, t=PACK),
-                z_f32[piece].rearrange("p t (c i) -> p c t i", i=4),
+                z_bf[:].rearrange("p (c i t) -> p c t i", i=LINE, t=PACK),
+                z_f32[h].rearrange("p t (c i) -> p c t i", i=LINE),
             )
-            h, within = divmod(start, HALF)
-            cols = slice(within, within + width)
-            nc.vector.quantize_mx(out=z_codes[h][:, cols].bitcast(FP8X4), scales=z_scales[h][:, cols], in_=z_bf[:])
+            nc.vector.quantize_mx(out=z_codes[h][:].bitcast(FP8X4), scales=z_scales[h][:], in_=z_bf[:])
 
         def score(h, t, words, scales, bank):
             rows = slice(t * P, (t + 1) * P)
@@ -175,9 +170,9 @@ def tile_picked_ccmpmaxbsum_none_p_kernel(
         def empty(h, bank, held, on_scalar):
             cols = slice(h * HALF, (h + 1) * HALF)
             if on_scalar:
-                nc.scalar.activation(held[:, cols], bank[:, cols], COPY, scale=0.0625)
+                nc.scalar.activation(held[:, cols], bank[:, cols], COPY, scale=SCORE_SCALE)
             else:
-                nc.vector.tensor_scalar_mul(held[:, cols], bank[:, cols], 0.0625)
+                nc.vector.tensor_scalar_mul(held[:, cols], bank[:, cols], SCORE_SCALE)
 
         quantise(0)
         for t in range(PACK):
@@ -185,70 +180,44 @@ def tile_picked_ccmpmaxbsum_none_p_kernel(
             score(0, t, a_words, a_scales, a_ps[t])
             empty(0, b_ps[t], b_sb[t], True)
             empty(0, a_ps[t], a_sb[t], True)
-        for piece in (1, 2):
-            for t in range(PACK):
-                mix(piece, t)
-            quantise(piece)
+        for t in range(PACK):
+            mix(1, t)
+        quantise(1)
         for t in range(PACK):
             score(1, t, b_words, b_scales, b_ps[t])
             empty(1, b_ps[t], b_sb[t], t == 0)
             score(1, t, a_words, a_scales, a_ps[t])
             empty(1, a_ps[t], a_sb[t], False)
 
-        a_at = [keep.tile([P, S], F32, name=f"a_at{t}") for t in range(PACK)]
-        b_at = [keep.tile([P, S], F32, name=f"b_at{t}") for t in range(PACK)]
-        for t, start in A_ON_VECTOR:
-            nc.vector.tensor_copy(a_at[t][:, start : start + HALF], a_sb[t][:].indirect(entries(n3_sb, start, HALF)))
+        a_shared = keep.tile([P, S], F32, name="a_shared")
+        nc.vector.tensor_copy(a_shared[:, :HALF], a_sb[SHARED_TILE][:].indirect(entries(n3_sb, 0, HALF)))
 
-        out_rows = out.rearrange("(g t b) j -> t g b j", t=PACK, b=RUN)
+        out_rows = out.rearrange("(p t) j -> p t j", t=PACK)
         for t in range(PACK):
             result = keep.tile([P, S], F32, name=f"result{t}")
             smaller = ring.tile([P, S], F32, name="smaller")
             larger = ring.tile([P, S], F32, name="larger")
+            a_at = ring.tile([P, S], F32, name="a_at") if t != SHARED_TILE else a_shared
+            b_at = ring.tile([P, S], F32, name="b_at")
 
-            def fetch_b(start, width):
-                window = b_sb[t][:].indirect(entries(n4_sb, start, width))
-                nc.scalar.activation(b_at[t][:, start : start + width], window, COPY)
+            def fetch(dst, held, offsets, start, width):
+                window = held[:].indirect(entries(offsets, start, width))
+                nc.scalar.activation(dst[:, start : start + width], window, COPY)
 
-            def fetch_a(start, width):
-                window = a_sb[t][:].indirect(entries(n3_sb, start, width))
-                nc.scalar.activation(a_at[t][:, start : start + width], window, COPY)
+            def combine(cols):
+                nc.vector.tensor_tensor(larger[:, cols], a_sb[t][:, cols], b_at[:, cols], ALU.max)
+                nc.vector.tensor_tensor(smaller[:, cols], a_at[:, cols], b_sb[t][:, cols], ALU.min)
+                nc.vector.tensor_tensor(result[:, cols], larger[:, cols], smaller[:, cols], ALU.subtract)
+                nc.sync.dma_start(out_rows[:, t, cols], result[:, cols])
 
-            def take_larger(cols):
-                nc.vector.scalar_tensor_tensor(
-                    larger[:, cols], a_ps[t][:, cols], 0.0625, b_at[t][:, cols], ALU.mult, ALU.max
-                )
-
-            def take_smaller(cols):
-                nc.vector.scalar_tensor_tensor(
-                    smaller[:, cols], b_ps[t][:, cols], 0.0625, a_at[t][:, cols], ALU.mult, ALU.min
-                )
-
-            def finish(cols, engine):
-                engine.tensor_tensor(result[:, cols], larger[:, cols], smaller[:, cols], ALU.subtract)
-                nc.sync.dma_start(out_rows[t][:, :, cols], result[:, cols])
-
-            whole = slice(0, S)
-            if t < 2:
-                for start, width in OUT_PIECES:
-                    fetch_b(start, width)
-                for start, width in OUT_PIECES:
-                    fetch_a(start, width)
-                take_larger(whole)
-                take_smaller(whole)
-                finish(whole, nc.gpsimd)
-            elif t == 2:
-                for start, width in OUT_PIECES:
-                    cols = slice(start, start + width)
-                    fetch_b(start, width)
-                    fetch_a(start, width)
-                    take_larger(cols)
-                    take_smaller(cols)
-                    finish(cols, nc.gpsimd if start == 0 else nc.vector)
+            if t < LAST:
+                for start, width in HALVES:
+                    fetch(b_at, b_sb[t], n4_sb, start, width)
+                for start, width in HALVES[1:] if t == SHARED_TILE else HALVES:
+                    fetch(a_at, a_sb[t], n3_sb, start, width)
+                combine(slice(0, S))
             else:
-                take_smaller(whole)
                 for start, width in LAST_PIECES:
-                    cols = slice(start, start + width)
-                    fetch_b(start, width)
-                    take_larger(cols)
-                    finish(cols, nc.vector)
+                    fetch(b_at, b_sb[t], n4_sb, start, width)
+                    fetch(a_at, a_sb[t], n3_sb, start, width)
+                    combine(slice(start, start + width))

from contextlib import ExitStack

import concourse.mybir as mybir

T, S, H, C = 2048, 512, 512, 512
FLOPS = 3 * 2 * 512 * 512 * 512

F32 = mybir.dt.float32
BF16 = mybir.dt.bfloat16
I32 = mybir.dt.int32
U32 = mybir.dt.uint32
U16 = mybir.dt.uint16
U8 = mybir.dt.uint8
FP8X4 = mybir.dt.float8_e4m3fn_x4
ALU = mybir.AluOpType
COPY = mybir.ActivationFunctionType.Copy

P = 128
PACK = 4
LAST = PACK - 1
HALF = S // 2
HALVES = ((0, HALF), (HALF, HALF))
LAST_PIECES = ((0, HALF), (HALF, HALF // 2), (HALF + HALF // 2, HALF // 2))
LINE = 4
SHARED_TILE = 1
SECOND_WEIGHT = 0.75
SCORE_SCALE = 0.0625


def entries(offsets, start, count):
    return offsets[:, start // 16 : (start + count) // 16]


def tile_picked_ccmpmaxbsum_none_p_kernel(
    tc, x_words, x_scales, w1, gs, offs, n1, n2, ca, cb, n3, n4, out
):
    nc = tc.nc
    with ExitStack() as ctx:
        keep = ctx.enter_context(tc.tile_pool(name="keep", bufs=1))
        ring = ctx.enter_context(tc.tile_pool(name="ring", bufs=PACK))
        psum = ctx.enter_context(tc.psum_pool(name="psum", bufs=1))

        def load_list(name, src):
            tile = keep.tile([P, S // 16], U16, name=name)
            nc.sync.dma_start(tile[:], src)
            return tile

        table_scales = keep.tile([P, T], U8, name="table_scales", align_bytes=64)
        nc.vector.memset(table_scales[:].bitcast(I32), 0)

        gs_sb = keep.tile([P, PACK], F32, name="gs_sb")
        nc.gpsimd.dma_start(gs_sb[:], gs.rearrange("(p t) o -> p (t o)", t=PACK))

        for r in range(4):
            nc.scalar.dma_start(table_scales[r:P:32, :].bitcast(I32), x_scales[0][r:16:4, :].bitcast(I32))
        offs_sb = load_list("offs_sb", offs)
        ca_sb = load_list("ca_sb", ca)
        cb_sb = load_list("cb_sb", cb)
        w_rows = w1.rearrange("(p j) c -> p j c", j=PACK)
        w_raw = []
        for h in range(2):
            raw = keep.tile([P, PACK, HALF], F32, name=f"w_raw{h}")
            nc.sync.dma_start(raw[:], w_rows[:, :, h * HALF : (h + 1) * HALF])
            w_raw.append(raw)
        table_words = keep.tile([P, T], U32, name="table_words", align_bytes=64)
        nc.sync.dma_start(table_words[:].bitcast(I32), x_words[0].rearrange("p n t -> p (n t)").bitcast(I32))
        n2_sb = load_list("n2_sb", n2)
        n1_sb = load_list("n1_sb", n1)
        n4_sb = load_list("n4_sb", n4)
        n3_sb = load_list("n3_sb", n3)

        def gather_dealt(dst, table, offsets):
            nc.vector.tensor_copy(dst[:].rearrange("p (t m) -> p m t", t=PACK), table[:].indirect(offsets[:]))

        tok_scales = keep.tile([P, S], U8, name="tok_scales", align_bytes=64)
        nc.vector.tensor_copy(tok_scales[:], table_scales[:].indirect(offs_sb[:]))
        a_scales = keep.tile([P, C], U8, name="a_scales", align_bytes=64)
        gather_dealt(a_scales, table_scales, ca_sb)
        b_scales = keep.tile([P, C], U8, name="b_scales", align_bytes=64)
        gather_dealt(b_scales, table_scales, cb_sb)

        w_bf = keep.tile([P, H * PACK], BF16, name="w_bf", align_bytes=64)
        w_bf_view = w_bf[:].rearrange("p (t m j) -> p m j t", t=PACK, j=PACK)
        for h in range(2):
            nc.scalar.activation(
                w_bf_view[:, h * HALF // PACK : (h + 1) * HALF // PACK],
                w_raw[h][:].rearrange("p j (m t) -> p m j t", t=PACK),
                COPY,
            )
        w_codes = keep.tile([P, H], U32, name="w_codes", align_bytes=64)
        w_scales = keep.tile([P, H], U8, name="w_scales", align_bytes=64)
        nc.vector.quantize_mx(out=w_codes[:].bitcast(FP8X4), scales=w_scales[:], in_=w_bf[:])

        tok_words = []
        for h in range(2):
            words = keep.tile([P, HALF], U32, name=f"tok_words{h}", align_bytes=64)
            nc.vector.tensor_copy(words[:], table_words[:].indirect(entries(offs_sb, h * HALF, HALF)))
            tok_words.append(words)
        a_words = keep.tile([P, C], U32, name="a_words", align_bytes=64)
        gather_dealt(a_words, table_words, ca_sb)
        b_words = keep.tile([P, C], U32, name="b_words", align_bytes=64)
        gather_dealt(b_words, table_words, cb_sb)

        y_sb = [keep.tile([P, S], F32, name=f"y_sb{t}") for t in range(PACK)]

        def project(h, t):
            rows = slice(t * P, (t + 1) * P)
            cols = slice(h * HALF, (h + 1) * HALF)
            bank = psum.tile([P, S], F32, name=f"y_ps{h}{t}", tag=f"bank{PACK * h + t}")
            nc.tensor.matmul_mx(
                bank[:, 0:HALF],
                lhsT=w_codes[:, rows].bitcast(FP8X4),
                lhsT_scale=w_scales[:, rows],
                rhs=tok_words[h][:].bitcast(FP8X4),
                rhs_scale=tok_scales[:, cols],
                start=True,
                stop=True,
            )
            if (h, t) != (1, LAST):
                nc.scalar.activation(y_sb[t][:, cols], bank[:, 0:HALF], COPY, scale=gs_sb[:, t : t + 1])
            else:
                nc.vector.tensor_scalar_mul(y_sb[t][:, cols], bank[:, 0:HALF], gs_sb[:, t : t + 1])

        z_room = keep.tile([P, (PACK + 1) * HALF], F32, name="z_room")
        z_f32 = [z_room[:, at : at + PACK * HALF].rearrange("p (t c) -> p t c", t=PACK) for at in (HALF, 0)]

        def mix(h, t):
            second = keep.tile([P, HALF], F32, name=f"second{h}{t}")
            nc.scalar.activation(
                second[:], y_sb[t][:].indirect(entries(n2_sb, h * HALF, HALF)), COPY, scale=SECOND_WEIGHT
            )
            nc.vector.tensor_tensor(
                z_f32[h][:, t, :], y_sb[t][:].indirect(entries(n1_sb, h * HALF, HALF)), second[:], ALU.add
            )

        for t in range(PACK):
            project(0, t)
        for t in range(PACK):
            project(1, t)
            mix(0, t)

        a_ps = [psum.tile([P, S], F32, name=f"a_ps{t}", tag=f"bank{2 * t}") for t in range(PACK)]
        b_ps = [psum.tile([P, S], F32, name=f"b_ps{t}", tag=f"bank{2 * t + 1}") for t in range(PACK)]
        a_sb = [keep.tile([P, S], F32, name=f"a_sb{t}") for t in range(PACK)]
        b_sb = [keep.tile([P, S], F32, name=f"b_sb{t}") for t in range(PACK)]

        z_codes = [keep.tile([P, HALF], U32, name=f"z_codes{h}", align_bytes=64) for h in range(2)]
        z_scales = [keep.tile([P, HALF], U8, name=f"z_scales{h}", align_bytes=64) for h in range(2)]

        def quantise(h):
            z_bf = keep.tile([P, HALF * PACK], BF16, name=f"z_bf{h}", align_bytes=64)
            nc.vector.tensor_copy(
                z_bf[:].rearrange("p (c i t) -> p c t i", i=LINE, t=PACK),
                z_f32[h].rearrange("p t (c i) -> p c t i", i=LINE),
            )
            nc.vector.quantize_mx(out=z_codes[h][:].bitcast(FP8X4), scales=z_scales[h][:], in_=z_bf[:])

        def score(h, t, words, scales, bank):
            rows = slice(t * P, (t + 1) * P)
            nc.tensor.matmul_mx(
                bank[:, h * HALF : (h + 1) * HALF],
                lhsT=words[:, rows].bitcast(FP8X4),
                lhsT_scale=scales[:, rows],
                rhs=z_codes[h][:].bitcast(FP8X4),
                rhs_scale=z_scales[h][:],
                start=True,
                stop=True,
            )

        def empty(h, bank, held, on_scalar):
            cols = slice(h * HALF, (h + 1) * HALF)
            if on_scalar:
                nc.scalar.activation(held[:, cols], bank[:, cols], COPY, scale=SCORE_SCALE)
            else:
                nc.vector.tensor_scalar_mul(held[:, cols], bank[:, cols], SCORE_SCALE)

        quantise(0)
        for t in range(PACK):
            score(0, t, b_words, b_scales, b_ps[t])
            score(0, t, a_words, a_scales, a_ps[t])
            empty(0, b_ps[t], b_sb[t], True)
            empty(0, a_ps[t], a_sb[t], True)
        for t in range(PACK):
            mix(1, t)
        quantise(1)
        for t in range(PACK):
            score(1, t, b_words, b_scales, b_ps[t])
            empty(1, b_ps[t], b_sb[t], t == 0)
            score(1, t, a_words, a_scales, a_ps[t])
            empty(1, a_ps[t], a_sb[t], False)

        a_shared = keep.tile([P, S], F32, name="a_shared")
        nc.vector.tensor_copy(a_shared[:, :HALF], a_sb[SHARED_TILE][:].indirect(entries(n3_sb, 0, HALF)))

        out_rows = out.rearrange("(p t) j -> p t j", t=PACK)
        for t in range(PACK):
            result = keep.tile([P, S], F32, name=f"result{t}")
            smaller = ring.tile([P, S], F32, name="smaller")
            larger = ring.tile([P, S], F32, name="larger")
            a_at = ring.tile([P, S], F32, name="a_at") if t != SHARED_TILE else a_shared
            b_at = ring.tile([P, S], F32, name="b_at")

            def fetch(dst, held, offsets, start, width):
                window = held[:].indirect(entries(offsets, start, width))
                nc.scalar.activation(dst[:, start : start + width], window, COPY)

            def combine(cols):
                nc.vector.tensor_tensor(larger[:, cols], a_sb[t][:, cols], b_at[:, cols], ALU.max)
                nc.vector.tensor_tensor(smaller[:, cols], a_at[:, cols], b_sb[t][:, cols], ALU.min)
                nc.vector.tensor_tensor(result[:, cols], larger[:, cols], smaller[:, cols], ALU.subtract)
                nc.sync.dma_start(out_rows[:, t, cols], result[:, cols])

            if t < LAST:
                for start, width in HALVES:
                    fetch(b_at, b_sb[t], n4_sb, start, width)
                for start, width in HALVES[1:] if t == SHARED_TILE else HALVES:
                    fetch(a_at, a_sb[t], n3_sb, start, width)
                combine(slice(0, S))
            else:
                for start, width in LAST_PIECES:
                    fetch(b_at, b_sb[t], n4_sb, start, width)
                    fetch(a_at, a_sb[t], n3_sb, start, width)
                    combine(slice(start, start + width))
